import numpy as np
import ml_dtypes


def mxq(x, axis, fmt="e4m3"):
    dtype, down = {"e4m3": (ml_dtypes.float8_e4m3fn, 7), "e5m2": (ml_dtypes.float8_e5m2, 14)}[fmt]
    v = np.moveaxis(np.asarray(x, np.float32).astype(ml_dtypes.bfloat16).astype(np.float64), axis, -1)
    blocks = v.reshape(v.shape[:-1] + (-1, 32))
    amax = np.abs(blocks).max(-1, keepdims=True)
    byte = np.maximum(np.where(amax > 0, np.frexp(amax)[1] - 1 + 127, 0) - down, 1)
    scale = np.exp2(byte - 127.0)
    codes = (blocks / scale).astype(np.float32).astype(dtype).astype(np.float64)
    return np.moveaxis((codes * scale).reshape(v.shape), -1, axis)


WIDE = False


def mx_kscale(k):
    if not WIDE:
        return np.ones(k)
    levels = np.array([10, -10, 5, -5, 0])
    if k % 512:
        return np.exp2(np.random.permutation(np.resize(levels, k // 32))).repeat(32)
    a = np.empty((k // 512, 16))
    for p in range(k // 512):
        a[p, :8] = np.random.permutation(np.resize(levels, 8))
        for g in range(8):
            far = levels[np.abs(levels - a[p, g]) >= 10]
            a[p, g + 8] = far[np.random.randint(len(far))]
    return np.exp2(a.ravel()).repeat(32)


def f64(x):
    return np.asarray(x).astype(np.float64)


def striped(idx):
    return np.tile(idx.reshape(-1, 16).T, (8, 1)).astype(np.uint16)


def unstriped(offs):
    return offs[:16].T.reshape(-1).astype(np.int64)


def striped8(idx):
    return np.concatenate([x.reshape(-1, 16).T for x in idx]).astype(np.uint16)


def runs(offs, k):
    lists = np.stack([offs[16 * r : 16 * r + 16].T.reshape(-1) for r in range(8)]).astype(np.int64)
    return lists[np.arange(k) % 512 // 64]


def pack_weight(w):
    k, n = w.shape
    w = f64(np.asarray(w, np.float32).astype(ml_dtypes.bfloat16)).reshape(k // 32, 32, n)
    amax = np.abs(w).max(1)
    byte = np.clip(np.where(amax > 0, np.frexp(amax)[1] - 1 + 127 - 7, 1), 1, 254)
    scaled = (w * np.exp2(127.0 - byte)[:, None, :]).reshape(k, n).astype(np.float32)
    words = np.ascontiguousarray(scaled.reshape(k // 512, 128, 4, n).transpose(0, 1, 3, 2)).astype(ml_dtypes.float8_e4m3fn).view(np.uint8)
    return words, np.ascontiguousarray(byte.astype(np.uint8).reshape(k // 512, 16, n))


def unpack_weight(words, scales):
    g, p, n, _ = words.shape
    vals = np.ascontiguousarray(words).view(ml_dtypes.float8_e4m3fn).astype(np.float64) * np.repeat(np.exp2(scales.astype(np.float64) - 127.0), 8, axis=1)[..., None]
    return vals.transpose(0, 1, 3, 2).reshape(g * 512, n)


K, T, S, V, N, H = 512, 2048, 512, 256, 512, 512


def setup_inputs():
    n = np.random.standard_normal
    s = mx_kscale(K)[:, None]
    u = mx_kscale(H)
    packed_xT = pack_weight(n((K, T)) * s)
    return {
        "x_words": packed_xT[0],
        "x_scales": packed_xT[1],
        "w1": (n((K, H)) / np.sqrt(K) / s).astype(np.float32),
        "gn": (np.random.uniform(0.5, 1.5, (H, 1)) * u[:, None]).astype(np.float32),
        "w2": (n((H, N)) / np.sqrt(H) / u[:, None]).astype(np.float32),
        "res": (2 * n((N, V))).astype(np.float32),
        "offs": striped(np.random.permutation(T)[:S]),
        "s1": striped8(np.stack([np.random.permutation(S)[:V] for _ in range(8)])),
        "s2": striped8(np.stack([np.random.permutation(S)[:V] for _ in range(8)])),
        "s3": striped8(np.stack([np.random.permutation(S)[:V] for _ in range(8)])),
        "s4": striped8(np.stack([np.random.permutation(S)[:V] for _ in range(8)])),
    }


def reference(x_words, x_scales, w1, gn, w2, res, offs, s1, s2, s3, s4):
    xq = unpack_weight(x_words, x_scales)[:, unstriped(offs)]
    y = np.tanh(mxq(f64(w1), 0, "e4m3").T @ xq)
    z = f64(gn) * (((y[np.arange(H)[:, None], runs(s1, H)]) * (y[np.arange(H)[:, None], runs(s2, H)])) * (y[np.arange(H)[:, None], runs(s3, H)] - (0.5 * (y[np.arange(H)[:, None], runs(s4, H)]))))
    return f64(res) + (mxq(f64(w2), 0, "e4m3").T @ mxq(z, 0, "e4m3"))

@@ -1,0 +1,168 @@
+from contextlib import ExitStack
+
+import concourse.mybir as mybir
+
+K, T, S, V, N, H = 512, 2048, 512, 256, 512, 512
+FLOPS = 2 * K * H * S + 2 * H * N * V
+
+F32 = mybir.dt.float32
+BF16 = mybir.dt.bfloat16
+I32 = mybir.dt.int32
+U32 = mybir.dt.uint32
+U16 = mybir.dt.uint16
+U8 = mybir.dt.uint8
+FP8X4 = mybir.dt.float8_e4m3fn_x4
+ACT = mybir.ActivationFunctionType
+ALU = mybir.AluOpType
+
+P = 128
+PACK = 4
+
+
+def tile_picked_plaq4_none_p_kernel(
+    tc, x_words, x_scales, w1, gn, w2, res, offs, s1, s2, s3, s4, out
+):
+    nc = tc.nc
+    with ExitStack() as ctx:
+        keep = ctx.enter_context(tc.tile_pool(name="keep", bufs=1))
+        psum = ctx.enter_context(tc.psum_pool(name="psum", bufs=1))
+
+        w1_raw = keep.tile([P, PACK, H], F32, name="w1_raw")
+        nc.sync.dma_start(out=w1_raw[:], in_=w1.rearrange("(p j) c -> p j c", j=PACK))
+        offs_sb = keep.tile([P, S // 16], U16, name="offs_sb")
+        nc.sync.dma_start(offs_sb[:], offs)
+        x_all = keep.tile([P, T], U32, name="x_all")
+        nc.sync.dma_start(
+            out=x_all[:].bitcast(I32), in_=x_words[0].rearrange("p n t -> p (n t)").bitcast(I32)
+        )
+        xs_all = keep.tile([P, T], U8, name="xs_all")
+        nc.vector.memset(xs_all[:].bitcast(I32), 0)
+        for q in range(4):
+            nc.scalar.dma_start(
+                out=xs_all[32 * q : 32 * q + 4, :].bitcast(I32),
+                in_=x_scales[0, 4 * q : 4 * q + 4, :].bitcast(I32),
+            )
+        HALF = N // 2
+        w2_rows = w2.rearrange("(p j) c -> p j c", j=PACK)
+        w2_raw = [keep.tile([P, PACK, HALF], F32, name="w2_raw%d" % h) for h in range(2)]
+        nc.sync.dma_start(out=w2_raw[0][:], in_=w2_rows[:, :, 0:HALF])
+        lists = []
+        for name, src in (("s1", s1), ("s2", s2), ("s3", s3), ("s4", s4)):
+            lst = keep.tile([P, V // 16], U16, name=name + "_sb")
+            nc.sync.dma_start(lst[:], src)
+            lists.append(lst)
+        l1, l2, l3, l4 = lists
+        gn_sb = keep.tile([P, PACK], F32, name="gn_sb")
+        nc.sync.dma_start(out=gn_sb[:], in_=gn.rearrange("(p t) o -> p (t o)", t=PACK))
+        nc.sync.dma_start(out=w2_raw[1][:], in_=w2_rows[:, :, HALF:N])
+        res_sb = keep.tile([P, PACK, V], F32, name="res_sb")
+        nc.sync.dma_start(out=res_sb[:], in_=res.rearrange("(j p) v -> p j v", p=P))
+
+        xs_pick = keep.tile([P, S], U8, name="xs_pick", align_bytes=64)
+        nc.vector.tensor_copy(xs_pick[:], xs_all[:].indirect(offs_sb[:]))
+
+        w1_src = w1_raw[:].rearrange("p j (m t) -> p m j t", t=PACK)
+        w1_codes = keep.tile([P, H], U32, name="w1_codes", align_bytes=64)
+        w1_scales = keep.tile([P, H], U8, name="w1_scales", align_bytes=64)
+        w1_bf = [keep.tile([P, 2, P, PACK], BF16, name="w1_bf%d" % u, align_bytes=64) for u in range(2)]
+        nc.vector.tensor_copy(out=w1_bf[0][:].rearrange("p t m j -> p m j t"), in_=w1_src[:, :, :, 0:2])
+        nc.scalar.copy(out=w1_bf[1][:].rearrange("p t m j -> p m j t"), in_=w1_src[:, :, :, 2:4])
+        for u in range(2):
+            cols = slice(2 * P * u, 2 * P * (u + 1))
+            nc.vector.quantize_mx(
+                out=w1_codes[:, cols].bitcast(FP8X4),
+                scales=w1_scales[:, cols],
+                in_=w1_bf[u][:].rearrange("p t m j -> p (t m j)"),
+            )
+
+        x_pick = keep.tile([P, S], U32, name="x_pick", align_bytes=64)
+        nc.vector.tensor_copy(x_pick[:], x_all[:].indirect(offs_sb[:]))
+
+        pre = [psum.tile([P, S], F32, name="pre%d" % t) for t in range(PACK)]
+        for t in range(PACK):
+            cols = slice(P * t, P * (t + 1))
+            nc.tensor.matmul_mx(
+                out=pre[t][:],
+                lhsT=w1_codes[:, cols].bitcast(FP8X4),
+                lhsT_scale=w1_scales[:, cols],
+                rhs=x_pick[:].bitcast(FP8X4),
+                rhs_scale=xs_pick[:],
+                start=True,
+                stop=True,
+            )
+
+        w2_bf = [keep.tile([P, HALF, PACK], BF16, name="w2_bf%d" % h, align_bytes=64) for h in range(2)]
+        w2_codes = [keep.tile([P, HALF], U32, name="w2_codes%d" % h, align_bytes=64) for h in range(2)]
+        w2_scales = [keep.tile([P, HALF], U8, name="w2_scales%d" % h, align_bytes=64) for h in range(2)]
+
+        def round_w2(h, copy):
+            copy(
+                out=w2_bf[h][:].rearrange("p (c i) j -> p c j i", i=4),
+                in_=w2_raw[h][:].rearrange("p j (c i) -> p c j i", i=4),
+            )
+
+        def quantise_w2(h):
+            nc.vector.quantize_mx(
+                out=w2_codes[h][:].bitcast(FP8X4),
+                scales=w2_scales[h][:],
+                in_=w2_bf[h][:].rearrange("p c j -> p (c j)"),
+            )
+
+        round_w2(0, nc.vector.tensor_copy)
+        quantise_w2(0)
+
+        z_rows = keep.tile([P, PACK, V], BF16, name="z_rows")
+        for t in range(PACK):
+            y = keep.tile([P, S], F32, name="y%d" % t)
+            nc.scalar.activation(y[:], pre[t][:], ACT.Tanh)
+            half4 = keep.tile([P, V], F32, name="half4_%d" % t)
+            nc.scalar.activation(half4[:], y[:].indirect(l4[:]), ACT.Copy, scale=-0.5)
+            y1 = keep.tile([P, V], F32, name="y1_%d" % t)
+            diff = keep.tile([P, V], F32, name="diff%d" % t)
+            prod = keep.tile([P, V], F32, name="prod%d" % t)
+            if t == 0:
+                nc.vector.tensor_copy(y1[:], y[:].indirect(l1[:]))
+                nc.vector.tensor_tensor(prod[:], y[:].indirect(l2[:]), y1[:], ALU.mult)
+                nc.vector.tensor_tensor(diff[:], y[:].indirect(l3[:]), half4[:], ALU.add)
+                other = diff
+            else:
+                nc.scalar.activation(y1[:], y[:].indirect(l1[:]), ACT.Copy)
+                nc.vector.tensor_tensor(diff[:], y[:].indirect(l3[:]), half4[:], ALU.add)
+                nc.vector.tensor_tensor(prod[:], y[:].indirect(l2[:]), diff[:], ALU.mult)
+                other = y1
+            nc.vector.scalar_tensor_tensor(
+                z_rows[:, t, :], prod[:], gn_sb[:, t : t + 1], other[:], ALU.mult, ALU.mult
+            )
+
+        round_w2(1, nc.scalar.copy)
+        quantise_w2(1)
+
+        z_bf = keep.tile([P, V, PACK], BF16, name="z_bf", align_bytes=64)
+        nc.vector.tensor_copy(
+            out=z_bf[:].rearrange("p (c i) t -> p c t i", i=4),
+            in_=z_rows[:].rearrange("p t (c i) -> p c t i", i=4),
+        )
+        z_codes = keep.tile([P, V], U32, name="z_codes", align_bytes=64)
+        z_scales = keep.tile([P, V], U8, name="z_scales", align_bytes=64)
+        nc.vector.quantize_mx(
+            out=z_codes[:].bitcast(FP8X4), scales=z_scales[:], in_=z_bf[:].rearrange("p v t -> p (v t)")
+        )
+
+        out_rows = out.rearrange("(j p) v -> p j v", p=P)
+        for h in range(2):
+            result = keep.tile([P, 2, V], F32, name="result%d" % h)
+            for i in range(2):
+                j = 2 * h + i
+                acc = psum.tile([P, V], F32, name="acc%d" % j)
+                cols = slice(P * i, P * (i + 1))
+                nc.tensor.matmul_mx(
+                    out=acc[:],
+                    lhsT=w2_codes[h][:, cols].bitcast(FP8X4),
+                    lhsT_scale=w2_scales[h][:, cols],
+                    rhs=z_codes[:].bitcast(FP8X4),
+                    rhs_scale=z_scales[:],
+                    start=True,
+                    stop=True,
+                )
+                nc.vector.tensor_tensor(result[:, i, :], acc[:], res_sb[:, j, :], ALU.add)
+            nc.sync.dma_start(out=out_rows[:, 2 * h : 2 * h + 2, :], in_=result[:])

@@ -27,31 +27,33 @@ def tile_picked_plaq4_none_p_kernel(
         keep = ctx.enter_context(tc.tile_pool(name="keep", bufs=1))
         psum = ctx.enter_context(tc.psum_pool(name="psum", bufs=1))
 
-        w1_raw = keep.tile([P, PACK, H], F32, name="w1_raw")
-        nc.sync.dma_start(out=w1_raw[:], in_=w1.rearrange("(p j) c -> p j c", j=PACK))
+        def load_list(name, src):
+            lst = keep.tile([P, V // 16], U16, name=name + "_sb")
+            nc.sync.dma_start(lst[:], src)
+            return lst
+
+        xs_all = keep.tile([P, T], U8, name="xs_all")
+        nc.vector.memset(xs_all[:, 0 : T // 2].bitcast(I32), 0)
+        nc.gpsimd.memset(xs_all[:, T // 2 : T].bitcast(I32), 0)
         offs_sb = keep.tile([P, S // 16], U16, name="offs_sb")
         nc.sync.dma_start(offs_sb[:], offs)
-        x_all = keep.tile([P, T], U32, name="x_all")
-        nc.sync.dma_start(
-            out=x_all[:].bitcast(I32), in_=x_words[0].rearrange("p n t -> p (n t)").bitcast(I32)
-        )
-        xs_all = keep.tile([P, T], U8, name="xs_all")
-        nc.vector.memset(xs_all[:].bitcast(I32), 0)
+        l4, l1 = load_list("s4", s4), load_list("s1", s1)
+        w1_raw = keep.tile([P, PACK, H], F32, name="w1_raw")
+        nc.sync.dma_start(out=w1_raw[:], in_=w1.rearrange("(p j) c -> p j c", j=PACK))
         for q in range(4):
-            nc.scalar.dma_start(
+            nc.sync.dma_start(
                 out=xs_all[32 * q : 32 * q + 4, :].bitcast(I32),
                 in_=x_scales[0, 4 * q : 4 * q + 4, :].bitcast(I32),
             )
+        l3, l2 = load_list("s3", s3), load_list("s2", s2)
+        x_all = keep.tile([P, T], U32, name="x_all", tag="x_all", align_bytes=64)
+        nc.sync.dma_start(
+            out=x_all[:].bitcast(I32), in_=x_words[0].rearrange("p n t -> p (n t)").bitcast(I32)
+        )
         HALF = N // 2
         w2_rows = w2.rearrange("(p j) c -> p j c", j=PACK)
         w2_raw = [keep.tile([P, PACK, HALF], F32, name="w2_raw%d" % h) for h in range(2)]
         nc.sync.dma_start(out=w2_raw[0][:], in_=w2_rows[:, :, 0:HALF])
-        lists = []
-        for name, src in (("s1", s1), ("s2", s2), ("s3", s3), ("s4", s4)):
-            lst = keep.tile([P, V // 16], U16, name=name + "_sb")
-            nc.sync.dma_start(lst[:], src)
-            lists.append(lst)
-        l1, l2, l3, l4 = lists
         gn_sb = keep.tile([P, PACK], F32, name="gn_sb")
         nc.sync.dma_start(out=gn_sb[:], in_=gn.rearrange("(p t) o -> p (t o)", t=PACK))
         nc.sync.dma_start(out=w2_raw[1][:], in_=w2_rows[:, :, HALF:N])
@@ -62,40 +64,53 @@ def tile_picked_plaq4_none_p_kernel(
         nc.vector.tensor_copy(xs_pick[:], xs_all[:].indirect(offs_sb[:]))
 
         w1_src = w1_raw[:].rearrange("p j (m t) -> p m j t", t=PACK)
-        w1_codes = keep.tile([P, H], U32, name="w1_codes", align_bytes=64)
-        w1_scales = keep.tile([P, H], U8, name="w1_scales", align_bytes=64)
         w1_bf = [keep.tile([P, 2, P, PACK], BF16, name="w1_bf%d" % u, align_bytes=64) for u in range(2)]
-        nc.vector.tensor_copy(out=w1_bf[0][:].rearrange("p t m j -> p m j t"), in_=w1_src[:, :, :, 0:2])
-        nc.scalar.copy(out=w1_bf[1][:].rearrange("p t m j -> p m j t"), in_=w1_src[:, :, :, 2:4])
         for u in range(2):
-            cols = slice(2 * P * u, 2 * P * (u + 1))
+            nc.scalar.copy(out=w1_bf[u][:].rearrange("p t m j -> p m j t"), in_=w1_src[:, :, :, 2 * u : 2 * u + 2])
+
+        def quantise_w1(u, tag):
+            codes = keep.tile([P, 2 * P], U32, name="w1_codes%d" % u, tag=tag, align_bytes=64)
+            scales = keep.tile([P, 2 * P], U8, name="w1_scales%d" % u, align_bytes=64)
             nc.vector.quantize_mx(
-                out=w1_codes[:, cols].bitcast(FP8X4),
-                scales=w1_scales[:, cols],
-                in_=w1_bf[u][:].rearrange("p t m j -> p (t m j)"),
+                out=codes[:].bitcast(FP8X4), scales=scales[:], in_=w1_bf[u][:].rearrange("p t m j -> p (t m j)")
             )
+            return codes, scales
+
+        w1_q = [quantise_w1(0, "w1_codes0")]
 
         x_pick = keep.tile([P, S], U32, name="x_pick", align_bytes=64)
-        nc.vector.tensor_copy(x_pick[:], x_all[:].indirect(offs_sb[:]))
-
-        pre = [psum.tile([P, S], F32, name="pre%d" % t) for t in range(PACK)]
-        for t in range(PACK):
-            cols = slice(P * t, P * (t + 1))
-            nc.tensor.matmul_mx(
-                out=pre[t][:],
-                lhsT=w1_codes[:, cols].bitcast(FP8X4),
-                lhsT_scale=w1_scales[:, cols],
-                rhs=x_pick[:].bitcast(FP8X4),
-                rhs_scale=xs_pick[:],
-                start=True,
-                stop=True,
+        link_pieces = (slice(0, 256), slice(256, 384), slice(384, 512))
+        for links in link_pieces:
+            nc.vector.tensor_copy(
+                x_pick[:, links], x_all[:].indirect(offs_sb[:, links.start // 16 : links.stop // 16])
             )
+        w1_q.append(quantise_w1(1, "x_all"))
 
-        w2_bf = [keep.tile([P, HALF, PACK], BF16, name="w2_bf%d" % h, align_bytes=64) for h in range(2)]
+        pre = []
+        for t in range(PACK):
+            w1_codes, w1_scales = w1_q[t // 2]
+            cols = slice(P * (t % 2), P * (t % 2 + 1))
+            pieces = []
+            for links in (link_pieces if t == 0 else (slice(0, S),)):
+                bank = psum.tile([P, links.stop - links.start], F32, name="pre%d_%d" % (t, links.start), tag="pre%d_%d" % (t, links.start))
+                nc.tensor.matmul_mx(
+                    out=bank[:],
+                    lhsT=w1_codes[:, cols].bitcast(FP8X4),
+                    lhsT_scale=w1_scales[:, cols],
+                    rhs=x_pick[:, links].bitcast(FP8X4),
+                    rhs_scale=xs_pick[:, links],
+                    start=True,
+                    stop=True,
+                )
+                pieces.append((links, bank))
+            pre.append(pieces)
+
+        w2_bf = {}
         w2_codes = [keep.tile([P, HALF], U32, name="w2_codes%d" % h, align_bytes=64) for h in range(2)]
         w2_scales = [keep.tile([P, HALF], U8, name="w2_scales%d" % h, align_bytes=64) for h in range(2)]
 
-        def round_w2(h, copy):
+        def round_w2(h, copy, tag):
+            w2_bf[h] = keep.tile([P, HALF, PACK], BF16, name="w2_bf%d" % h, tag=tag, align_bytes=64)
             copy(
                 out=w2_bf[h][:].rearrange("p (c i) j -> p c j i", i=4),
                 in_=w2_raw[h][:].rearrange("p j (c i) -> p c j i", i=4),
@@ -108,33 +123,38 @@ def tile_picked_plaq4_none_p_kernel(
                 in_=w2_bf[h][:].rearrange("p c j -> p (c j)"),
             )
 
-        round_w2(0, nc.vector.tensor_copy)
+        round_w2(0, nc.vector.tensor_copy, "w2_bf0")
         quantise_w2(0)
 
         z_rows = keep.tile([P, PACK, V], BF16, name="z_rows")
+        pending = []
+
+        def finish(t, diff, prod):
+            nc.vector.scalar_tensor_tensor(
+                z_rows[:, t, :], diff[:], gn_sb[:, t : t + 1], prod[:], ALU.mult, ALU.mult
+            )
+
         for t in range(PACK):
             y = keep.tile([P, S], F32, name="y%d" % t)
-            nc.scalar.activation(y[:], pre[t][:], ACT.Tanh)
-            half4 = keep.tile([P, V], F32, name="half4_%d" % t)
+            for links, bank in pre[t]:
+                nc.scalar.activation(y[:, links], bank[:], ACT.Tanh)
+            half4 = keep.tile([P, V], F32, name="half4_%d" % t, tag="half4_%d" % t, align_bytes=64)
             nc.scalar.activation(half4[:], y[:].indirect(l4[:]), ACT.Copy, scale=-0.5)
             y1 = keep.tile([P, V], F32, name="y1_%d" % t)
             diff = keep.tile([P, V], F32, name="diff%d" % t)
             prod = keep.tile([P, V], F32, name="prod%d" % t)
             if t == 0:
                 nc.vector.tensor_copy(y1[:], y[:].indirect(l1[:]))
-                nc.vector.tensor_tensor(prod[:], y[:].indirect(l2[:]), y1[:], ALU.mult)
-                nc.vector.tensor_tensor(diff[:], y[:].indirect(l3[:]), half4[:], ALU.add)
-                other = diff
             else:
                 nc.scalar.activation(y1[:], y[:].indirect(l1[:]), ACT.Copy)
-                nc.vector.tensor_tensor(diff[:], y[:].indirect(l3[:]), half4[:], ALU.add)
-                nc.vector.tensor_tensor(prod[:], y[:].indirect(l2[:]), diff[:], ALU.mult)
-                other = y1
-            nc.vector.scalar_tensor_tensor(
-                z_rows[:, t, :], prod[:], gn_sb[:, t : t + 1], other[:], ALU.mult, ALU.mult
-            )
+            nc.vector.tensor_tensor(diff[:], y[:].indirect(l3[:]), half4[:], ALU.add)
+            if pending:
+                finish(*pending[-1])
+            nc.vector.tensor_tensor(prod[:], y[:].indirect(l2[:]), y1[:], ALU.mult)
+            pending.append((t, diff, prod))
+        finish(*pending[-1])
 
-        round_w2(1, nc.scalar.copy)
+        round_w2(1, nc.scalar.copy, "half4_2")
         quantise_w2(1)
 
         z_bf = keep.tile([P, V, PACK], BF16, name="z_bf", align_bytes=64)
@@ -149,20 +169,20 @@ def tile_picked_plaq4_none_p_kernel(
         )
 
         out_rows = out.rearrange("(j p) v -> p j v", p=P)
-        for h in range(2):
-            result = keep.tile([P, 2, V], F32, name="result%d" % h)
-            for i in range(2):
-                j = 2 * h + i
-                acc = psum.tile([P, V], F32, name="acc%d" % j)
-                cols = slice(P * i, P * (i + 1))
-                nc.tensor.matmul_mx(
-                    out=acc[:],
-                    lhsT=w2_codes[h][:, cols].bitcast(FP8X4),
-                    lhsT_scale=w2_scales[h][:, cols],
-                    rhs=z_codes[:].bitcast(FP8X4),
-                    rhs_scale=z_scales[:],
-                    start=True,
-                    stop=True,
-                )
-                nc.vector.tensor_tensor(result[:, i, :], acc[:], res_sb[:, j, :], ALU.add)
-            nc.sync.dma_start(out=out_rows[:, 2 * h : 2 * h + 2, :], in_=result[:])
+        for j in range(PACK):
+            h, i = divmod(j, 2)
+            result = keep.tile([P, V], F32, name="result%d" % j)
+            acc = psum.tile([P, V], F32, name="acc%d" % j, tag="pre%d_0" % j)
+            cols = slice(P * i, P * (i + 1))
+            nc.tensor.matmul_mx(
+                out=acc[:],
+                lhsT=w2_codes[h][:, cols].bitcast(FP8X4),
+                lhsT_scale=w2_scales[h][:, cols],
+                rhs=z_codes[:].bitcast(FP8X4),
+                rhs_scale=z_scales[:],
+                start=True,
+                stop=True,
+            )
+            nc.vector.tensor_tensor(result[:], acc[:], res_sb[:, j, :], ALU.add)
+            queue = nc.scalar if j % 2 == 0 else nc.sync
+            queue.dma_start(out=out_rows[:, j, :], in_=result[:])

@@ -65,8 +65,8 @@ def tile_picked_plaq4_none_p_kernel(
 
         w1_src = w1_raw[:].rearrange("p j (m t) -> p m j t", t=PACK)
         w1_bf = [keep.tile([P, 2, P, PACK], BF16, name="w1_bf%d" % u, align_bytes=64) for u in range(2)]
-        for u in range(2):
-            nc.scalar.copy(out=w1_bf[u][:].rearrange("p t m j -> p m j t"), in_=w1_src[:, :, :, 2 * u : 2 * u + 2])
+        for u, copy in enumerate((nc.scalar.copy, nc.vector.tensor_copy)):
+            copy(out=w1_bf[u][:].rearrange("p t m j -> p m j t"), in_=w1_src[:, :, :, 2 * u : 2 * u + 2])
 
         def quantise_w1(u, tag):
             codes = keep.tile([P, 2 * P], U32, name="w1_codes%d" % u, tag=tag, align_bytes=64)
@@ -106,7 +106,7 @@ def tile_picked_plaq4_none_p_kernel(
             pre.append(pieces)
 
         w2_bf = {}
-        w2_codes = [keep.tile([P, HALF], U32, name="w2_codes%d" % h, align_bytes=64) for h in range(2)]
+        w2_codes = {}
         w2_scales = [keep.tile([P, HALF], U8, name="w2_scales%d" % h, align_bytes=64) for h in range(2)]
 
         def round_w2(h, copy, tag):
@@ -116,7 +116,8 @@ def tile_picked_plaq4_none_p_kernel(
                 in_=w2_raw[h][:].rearrange("p j (c i) -> p c j i", i=4),
             )
 
-        def quantise_w2(h):
+        def quantise_w2(h, tag):
+            w2_codes[h] = keep.tile([P, HALF], U32, name="w2_codes%d" % h, tag=tag, align_bytes=64)
             nc.vector.quantize_mx(
                 out=w2_codes[h][:].bitcast(FP8X4),
                 scales=w2_scales[h][:],
@@ -124,49 +125,52 @@ def tile_picked_plaq4_none_p_kernel(
             )
 
         round_w2(0, nc.vector.tensor_copy, "w2_bf0")
-        quantise_w2(0)
+        quantise_w2(0, "w2_codes0")
 
-        z_rows = keep.tile([P, PACK, V], BF16, name="z_rows")
-        pending = []
+        z_pairs = [keep.tile([P, 2, V], BF16, name="z_pair%d" % u) for u in range(2)]
+        y, y1, diff, prod = {}, {}, {}, {}
 
-        def finish(t, diff, prod):
+        def finish(t):
             nc.vector.scalar_tensor_tensor(
-                z_rows[:, t, :], diff[:], gn_sb[:, t : t + 1], prod[:], ALU.mult, ALU.mult
+                z_pairs[t // 2][:, t % 2, :], diff[t][:], gn_sb[:, t : t + 1], prod[t][:], ALU.mult, ALU.mult
             )
 
+        LATE = 2
         for t in range(PACK):
-            y = keep.tile([P, S], F32, name="y%d" % t)
+            y[t] = keep.tile([P, S], F32, name="y%d" % t)
             for links, bank in pre[t]:
-                nc.scalar.activation(y[:, links], bank[:], ACT.Tanh)
+                nc.scalar.activation(y[t][:, links], bank[:], ACT.Tanh)
             half4 = keep.tile([P, V], F32, name="half4_%d" % t, tag="half4_%d" % t, align_bytes=64)
-            nc.scalar.activation(half4[:], y[:].indirect(l4[:]), ACT.Copy, scale=-0.5)
-            y1 = keep.tile([P, V], F32, name="y1_%d" % t)
-            diff = keep.tile([P, V], F32, name="diff%d" % t)
-            prod = keep.tile([P, V], F32, name="prod%d" % t)
+            nc.scalar.activation(half4[:], y[t][:].indirect(l4[:]), ACT.Copy, scale=-0.5)
+            y1[t] = keep.tile([P, V], F32, name="y1_%d" % t)
+            diff[t] = keep.tile([P, V], F32, name="diff%d" % t)
+            prod[t] = keep.tile([P, V], F32, name="prod%d" % t)
             if t == 0:
-                nc.vector.tensor_copy(y1[:], y[:].indirect(l1[:]))
+                nc.vector.tensor_copy(y1[t][:], y[t][:].indirect(l1[:]))
             else:
-                nc.scalar.activation(y1[:], y[:].indirect(l1[:]), ACT.Copy)
-            nc.vector.tensor_tensor(diff[:], y[:].indirect(l3[:]), half4[:], ALU.add)
-            if pending:
-                finish(*pending[-1])
-            nc.vector.tensor_tensor(prod[:], y[:].indirect(l2[:]), y1[:], ALU.mult)
-            pending.append((t, diff, prod))
-        finish(*pending[-1])
+                nc.scalar.activation(y1[t][:], y[t][:].indirect(l1[:]), ACT.Copy)
+            nc.vector.tensor_tensor(diff[t][:], y[t][:].indirect(l3[:]), half4[:], ALU.add)
+            if t > 0 and t - 1 != LATE:
+                finish(t - 1)
+            if t != LATE:
+                nc.vector.tensor_tensor(prod[t][:], y[t][:].indirect(l2[:]), y1[t][:], ALU.mult)
+        y2_late = keep.tile([P, V], F32, name="y2_late")
+        nc.scalar.activation(y2_late[:], y[LATE][:].indirect(l2[:]), ACT.Copy)
+        finish(PACK - 1)
+        nc.vector.tensor_tensor(prod[LATE][:], y2_late[:], y1[LATE][:], ALU.mult)
+        finish(LATE)
 
+        z_bf = keep.tile([P, V, PACK], BF16, name="z_bf", tag="z_bf", align_bytes=64)
+        for u, copy in enumerate((nc.scalar.copy, nc.vector.tensor_copy)):
+            copy(out=z_bf[:, :, 2 * u : 2 * u + 2], in_=z_pairs[u][:].rearrange("p t v -> p v t"))
         round_w2(1, nc.scalar.copy, "half4_2")
-        quantise_w2(1)
-
-        z_bf = keep.tile([P, V, PACK], BF16, name="z_bf", align_bytes=64)
-        nc.vector.tensor_copy(
-            out=z_bf[:].rearrange("p (c i) t -> p c t i", i=4),
-            in_=z_rows[:].rearrange("p t (c i) -> p c t i", i=4),
-        )
         z_codes = keep.tile([P, V], U32, name="z_codes", align_bytes=64)
         z_scales = keep.tile([P, V], U8, name="z_scales", align_bytes=64)
         nc.vector.quantize_mx(
             out=z_codes[:].bitcast(FP8X4), scales=z_scales[:], in_=z_bf[:].rearrange("p v t -> p (v t)")
         )
+
+        quantise_w2(1, "z_bf")
 
         out_rows = out.rearrange("(j p) v -> p j v", p=P)
         for j in range(PACK):

@@ -17,6 +17,14 @@ ALU = mybir.AluOpType
 
 P = 128
 PACK = 4
+GROUP = 16
+LINE = 4
+W2_HALF = N // 2
+
+LINK_PIECES = (slice(0, 256), slice(256, 384), slice(384, 512))
+
+FIRST_PLANE = 0
+LATE_PLANE = 2
 
 
 def tile_picked_plaq4_none_p_kernel(
@@ -28,14 +36,14 @@ def tile_picked_plaq4_none_p_kernel(
         psum = ctx.enter_context(tc.psum_pool(name="psum", bufs=1))
 
         def load_list(name, src):
-            lst = keep.tile([P, V // 16], U16, name=name + "_sb")
+            lst = keep.tile([P, V // GROUP], U16, name=name + "_sb")
             nc.sync.dma_start(lst[:], src)
             return lst
 
         xs_all = keep.tile([P, T], U8, name="xs_all")
         nc.vector.memset(xs_all[:, 0 : T // 2].bitcast(I32), 0)
         nc.gpsimd.memset(xs_all[:, T // 2 : T].bitcast(I32), 0)
-        offs_sb = keep.tile([P, S // 16], U16, name="offs_sb")
+        offs_sb = keep.tile([P, S // GROUP], U16, name="offs_sb")
         nc.sync.dma_start(offs_sb[:], offs)
         l4, l1 = load_list("s4", s4), load_list("s1", s1)
         w1_raw = keep.tile([P, PACK, H], F32, name="w1_raw")
@@ -50,23 +58,22 @@ def tile_picked_plaq4_none_p_kernel(
         nc.sync.dma_start(
             out=x_all[:].bitcast(I32), in_=x_words[0].rearrange("p n t -> p (n t)").bitcast(I32)
         )
-        HALF = N // 2
         w2_rows = w2.rearrange("(p j) c -> p j c", j=PACK)
-        w2_raw = [keep.tile([P, PACK, HALF], F32, name="w2_raw%d" % h) for h in range(2)]
-        nc.sync.dma_start(out=w2_raw[0][:], in_=w2_rows[:, :, 0:HALF])
+        w2_raw = [keep.tile([P, PACK, W2_HALF], F32, name="w2_raw%d" % h) for h in range(2)]
+        nc.sync.dma_start(out=w2_raw[0][:], in_=w2_rows[:, :, 0:W2_HALF])
         gn_sb = keep.tile([P, PACK], F32, name="gn_sb")
         nc.sync.dma_start(out=gn_sb[:], in_=gn.rearrange("(p t) o -> p (t o)", t=PACK))
-        nc.sync.dma_start(out=w2_raw[1][:], in_=w2_rows[:, :, HALF:N])
-        res_sb = keep.tile([P, PACK, V], F32, name="res_sb")
-        nc.sync.dma_start(out=res_sb[:], in_=res.rearrange("(j p) v -> p j v", p=P))
+        nc.sync.dma_start(out=w2_raw[1][:], in_=w2_rows[:, :, W2_HALF:N])
+        res_sb = keep.tile([P, N // P, V], F32, name="res_sb")
+        nc.sync.dma_start(out=res_sb[:], in_=res.rearrange("(b p) v -> p b v", p=P))
 
         xs_pick = keep.tile([P, S], U8, name="xs_pick", align_bytes=64)
         nc.vector.tensor_copy(xs_pick[:], xs_all[:].indirect(offs_sb[:]))
 
-        w1_src = w1_raw[:].rearrange("p j (m t) -> p m j t", t=PACK)
+        w1_dealt = w1_raw[:].rearrange("p j (m t) -> p m j t", t=PACK)
         w1_bf = [keep.tile([P, 2, P, PACK], BF16, name="w1_bf%d" % u, align_bytes=64) for u in range(2)]
         for u, copy in enumerate((nc.scalar.copy, nc.vector.tensor_copy)):
-            copy(out=w1_bf[u][:].rearrange("p t m j -> p m j t"), in_=w1_src[:, :, :, 2 * u : 2 * u + 2])
+            copy(out=w1_bf[u][:].rearrange("p t m j -> p m j t"), in_=w1_dealt[:, :, :, 2 * u : 2 * u + 2])
 
         def quantise_w1(u, tag):
             codes = keep.tile([P, 2 * P], U32, name="w1_codes%d" % u, tag=tag, align_bytes=64)
@@ -79,10 +86,9 @@ def tile_picked_plaq4_none_p_kernel(
         w1_q = [quantise_w1(0, "w1_codes0")]
 
         x_pick = keep.tile([P, S], U32, name="x_pick", align_bytes=64)
-        link_pieces = (slice(0, 256), slice(256, 384), slice(384, 512))
-        for links in link_pieces:
+        for links in LINK_PIECES:
             nc.vector.tensor_copy(
-                x_pick[:, links], x_all[:].indirect(offs_sb[:, links.start // 16 : links.stop // 16])
+                x_pick[:, links], x_all[:].indirect(offs_sb[:, links.start // GROUP : links.stop // GROUP])
             )
         w1_q.append(quantise_w1(1, "x_all"))
 
@@ -91,8 +97,9 @@ def tile_picked_plaq4_none_p_kernel(
             w1_codes, w1_scales = w1_q[t // 2]
             cols = slice(P * (t % 2), P * (t % 2 + 1))
             pieces = []
-            for links in (link_pieces if t == 0 else (slice(0, S),)):
-                bank = psum.tile([P, links.stop - links.start], F32, name="pre%d_%d" % (t, links.start), tag="pre%d_%d" % (t, links.start))
+            for links in LINK_PIECES if t == FIRST_PLANE else (slice(0, S),):
+                bank_name = "pre%d_%d" % (t, links.start)
+                bank = psum.tile([P, links.stop - links.start], F32, name=bank_name, tag=bank_name)
                 nc.tensor.matmul_mx(
                     out=bank[:],
                     lhsT=w1_codes[:, cols].bitcast(FP8X4),
@@ -105,26 +112,25 @@ def tile_picked_plaq4_none_p_kernel(
                 pieces.append((links, bank))
             pre.append(pieces)
 
-        w2_bf = {}
-        w2_codes = {}
-        w2_scales = [keep.tile([P, HALF], U8, name="w2_scales%d" % h, align_bytes=64) for h in range(2)]
+        w2_bf, w2_codes = {}, {}
+        w2_scales = [keep.tile([P, W2_HALF], U8, name="w2_scales%d" % h, align_bytes=64) for h in range(2)]
 
-        def round_w2(h, copy, tag):
-            w2_bf[h] = keep.tile([P, HALF, PACK], BF16, name="w2_bf%d" % h, tag=tag, align_bytes=64)
+        def round_w2(h, copy):
+            w2_bf[h] = keep.tile([P, W2_HALF, PACK], BF16, name="w2_bf%d" % h, align_bytes=64)
             copy(
-                out=w2_bf[h][:].rearrange("p (c i) j -> p c j i", i=4),
-                in_=w2_raw[h][:].rearrange("p j (c i) -> p c j i", i=4),
+                out=w2_bf[h][:].rearrange("p (c i) j -> p c j i", i=LINE),
+                in_=w2_raw[h][:].rearrange("p j (c i) -> p c j i", i=LINE),
             )
 
         def quantise_w2(h, tag):
-            w2_codes[h] = keep.tile([P, HALF], U32, name="w2_codes%d" % h, tag=tag, align_bytes=64)
+            w2_codes[h] = keep.tile([P, W2_HALF], U32, name="w2_codes%d" % h, tag=tag, align_bytes=64)
             nc.vector.quantize_mx(
                 out=w2_codes[h][:].bitcast(FP8X4),
                 scales=w2_scales[h][:],
                 in_=w2_bf[h][:].rearrange("p c j -> p (c j)"),
             )
 
-        round_w2(0, nc.vector.tensor_copy, "w2_bf0")
+        round_w2(0, nc.vector.tensor_copy)
         quantise_w2(0, "w2_codes0")
 
         z_pairs = [keep.tile([P, 2, V], BF16, name="z_pair%d" % u) for u in range(2)]
@@ -135,48 +141,51 @@ def tile_picked_plaq4_none_p_kernel(
                 z_pairs[t // 2][:, t % 2, :], diff[t][:], gn_sb[:, t : t + 1], prod[t][:], ALU.mult, ALU.mult
             )
 
-        LATE = 2
         for t in range(PACK):
             y[t] = keep.tile([P, S], F32, name="y%d" % t)
             for links, bank in pre[t]:
                 nc.scalar.activation(y[t][:, links], bank[:], ACT.Tanh)
-            half4 = keep.tile([P, V], F32, name="half4_%d" % t, tag="half4_%d" % t, align_bytes=64)
+            half4 = keep.tile([P, V], F32, name="half4_%d" % t)
             nc.scalar.activation(half4[:], y[t][:].indirect(l4[:]), ACT.Copy, scale=-0.5)
             y1[t] = keep.tile([P, V], F32, name="y1_%d" % t)
             diff[t] = keep.tile([P, V], F32, name="diff%d" % t)
             prod[t] = keep.tile([P, V], F32, name="prod%d" % t)
-            if t == 0:
+            if t == FIRST_PLANE:
                 nc.vector.tensor_copy(y1[t][:], y[t][:].indirect(l1[:]))
-            else:
+            elif t != LATE_PLANE:
                 nc.scalar.activation(y1[t][:], y[t][:].indirect(l1[:]), ACT.Copy)
             nc.vector.tensor_tensor(diff[t][:], y[t][:].indirect(l3[:]), half4[:], ALU.add)
-            if t > 0 and t - 1 != LATE:
+            if t > 0 and t - 1 != LATE_PLANE:
                 finish(t - 1)
-            if t != LATE:
+            if t != LATE_PLANE:
                 nc.vector.tensor_tensor(prod[t][:], y[t][:].indirect(l2[:]), y1[t][:], ALU.mult)
+
+        late = LATE_PLANE
+        nc.scalar.activation(y1[late][:], y[late][:].indirect(l1[:]), ACT.Copy)
         y2_late = keep.tile([P, V], F32, name="y2_late")
-        nc.scalar.activation(y2_late[:], y[LATE][:].indirect(l2[:]), ACT.Copy)
+        nc.scalar.activation(y2_late[:], y[late][:].indirect(l2[:]), ACT.Copy)
+        nc.vector.scalar_tensor_tensor(
+            prod[late][:], diff[late][:], gn_sb[:, late : late + 1], y1[late][:], ALU.mult, ALU.mult
+        )
         finish(PACK - 1)
-        nc.vector.tensor_tensor(prod[LATE][:], y2_late[:], y1[LATE][:], ALU.mult)
-        finish(LATE)
+        nc.vector.tensor_tensor(z_pairs[late // 2][:, late % 2, :], prod[late][:], y2_late[:], ALU.mult)
 
         z_bf = keep.tile([P, V, PACK], BF16, name="z_bf", tag="z_bf", align_bytes=64)
         for u, copy in enumerate((nc.scalar.copy, nc.vector.tensor_copy)):
             copy(out=z_bf[:, :, 2 * u : 2 * u + 2], in_=z_pairs[u][:].rearrange("p t v -> p v t"))
-        round_w2(1, nc.scalar.copy, "half4_2")
+        round_w2(1, nc.scalar.copy)
         z_codes = keep.tile([P, V], U32, name="z_codes", align_bytes=64)
         z_scales = keep.tile([P, V], U8, name="z_scales", align_bytes=64)
         nc.vector.quantize_mx(
             out=z_codes[:].bitcast(FP8X4), scales=z_scales[:], in_=z_bf[:].rearrange("p v t -> p (v t)")
         )
-
         quantise_w2(1, "z_bf")
 
-        out_rows = out.rearrange("(j p) v -> p j v", p=P)
-        for j in range(PACK):
-            h, i = divmod(j, 2)
-            result = keep.tile([P, V], F32, name="result%d" % j)
-            acc = psum.tile([P, V], F32, name="acc%d" % j, tag="pre%d_0" % j)
+        out_rows = out.rearrange("(b p) v -> p b v", p=P)
+        for b in range(N // P):
+            h, i = divmod(b, W2_HALF // P)
+            result = keep.tile([P, V], F32, name="result%d" % b)
+            acc = psum.tile([P, V], F32, name="acc%d" % b, tag="pre%d_0" % b)
             cols = slice(P * i, P * (i + 1))
             nc.tensor.matmul_mx(
                 out=acc[:],
@@ -187,6 +196,6 @@ def tile_picked_plaq4_none_p_kernel(
                 start=True,
                 stop=True,
             )
-            nc.vector.tensor_tensor(result[:], acc[:], res_sb[:, j, :], ALU.add)
-            queue = nc.scalar if j % 2 == 0 else nc.sync
-            queue.dma_start(out=out_rows[:, j, :], in_=result[:])
+            nc.vector.tensor_tensor(result[:], acc[:], res_sb[:, b, :], ALU.add)
+            queue = nc.scalar if b % 2 == 0 else nc.sync
+            queue.dma_start(out=out_rows[:, b, :], in_=result[:])

from contextlib import ExitStack

import concourse.mybir as mybir

K, T, S, V, N, H = 512, 2048, 512, 256, 512, 512
FLOPS = 2 * K * H * S + 2 * H * N * V

F32 = mybir.dt.float32
BF16 = mybir.dt.bfloat16
I32 = mybir.dt.int32
U32 = mybir.dt.uint32
U16 = mybir.dt.uint16
U8 = mybir.dt.uint8
FP8X4 = mybir.dt.float8_e4m3fn_x4
ACT = mybir.ActivationFunctionType
ALU = mybir.AluOpType

P = 128
PACK = 4
GROUP = 16
LINE = 4
W2_HALF = N // 2

LINK_PIECES = (slice(0, 256), slice(256, 384), slice(384, 512))

FIRST_PLANE = 0
LATE_PLANE = 2


def tile_picked_plaq4_none_p_kernel(
    tc, x_words, x_scales, w1, gn, w2, res, offs, s1, s2, s3, s4, out
):
    nc = tc.nc
    with ExitStack() as ctx:
        keep = ctx.enter_context(tc.tile_pool(name="keep", bufs=1))
        psum = ctx.enter_context(tc.psum_pool(name="psum", bufs=1))

        def load_list(name, src):
            lst = keep.tile([P, V // GROUP], U16, name=name + "_sb")
            nc.sync.dma_start(lst[:], src)
            return lst

        xs_all = keep.tile([P, T], U8, name="xs_all")
        nc.vector.memset(xs_all[:, 0 : T // 2].bitcast(I32), 0)
        nc.gpsimd.memset(xs_all[:, T // 2 : T].bitcast(I32), 0)
        offs_sb = keep.tile([P, S // GROUP], U16, name="offs_sb")
        nc.sync.dma_start(offs_sb[:], offs)
        l4, l1 = load_list("s4", s4), load_list("s1", s1)
        w1_raw = keep.tile([P, PACK, H], F32, name="w1_raw")
        nc.sync.dma_start(out=w1_raw[:], in_=w1.rearrange("(p j) c -> p j c", j=PACK))
        for q in range(4):
            nc.sync.dma_start(
                out=xs_all[32 * q : 32 * q + 4, :].bitcast(I32),
                in_=x_scales[0, 4 * q : 4 * q + 4, :].bitcast(I32),
            )
        l3, l2 = load_list("s3", s3), load_list("s2", s2)
        x_all = keep.tile([P, T], U32, name="x_all", tag="x_all", align_bytes=64)
        nc.sync.dma_start(
            out=x_all[:].bitcast(I32), in_=x_words[0].rearrange("p n t -> p (n t)").bitcast(I32)
        )
        w2_rows = w2.rearrange("(p j) c -> p j c", j=PACK)
        w2_raw = [keep.tile([P, PACK, W2_HALF], F32, name="w2_raw%d" % h) for h in range(2)]
        nc.sync.dma_start(out=w2_raw[0][:], in_=w2_rows[:, :, 0:W2_HALF])
        gn_sb = keep.tile([P, PACK], F32, name="gn_sb")
        nc.sync.dma_start(out=gn_sb[:], in_=gn.rearrange("(p t) o -> p (t o)", t=PACK))
        nc.sync.dma_start(out=w2_raw[1][:], in_=w2_rows[:, :, W2_HALF:N])
        res_sb = keep.tile([P, N // P, V], F32, name="res_sb")
        nc.sync.dma_start(out=res_sb[:], in_=res.rearrange("(b p) v -> p b v", p=P))

        xs_pick = keep.tile([P, S], U8, name="xs_pick", align_bytes=64)
        nc.vector.tensor_copy(xs_pick[:], xs_all[:].indirect(offs_sb[:]))

        w1_dealt = w1_raw[:].rearrange("p j (m t) -> p m j t", t=PACK)
        w1_bf = [keep.tile([P, 2, P, PACK], BF16, name="w1_bf%d" % u, align_bytes=64) for u in range(2)]
        for u, copy in enumerate((nc.scalar.copy, nc.vector.tensor_copy)):
            copy(out=w1_bf[u][:].rearrange("p t m j -> p m j t"), in_=w1_dealt[:, :, :, 2 * u : 2 * u + 2])

        def quantise_w1(u, tag):
            codes = keep.tile([P, 2 * P], U32, name="w1_codes%d" % u, tag=tag, align_bytes=64)
            scales = keep.tile([P, 2 * P], U8, name="w1_scales%d" % u, align_bytes=64)
            nc.vector.quantize_mx(
                out=codes[:].bitcast(FP8X4), scales=scales[:], in_=w1_bf[u][:].rearrange("p t m j -> p (t m j)")
            )
            return codes, scales

        w1_q = [quantise_w1(0, "w1_codes0")]

        x_pick = keep.tile([P, S], U32, name="x_pick", align_bytes=64)
        for links in LINK_PIECES:
            nc.vector.tensor_copy(
                x_pick[:, links], x_all[:].indirect(offs_sb[:, links.start // GROUP : links.stop // GROUP])
            )
        w1_q.append(quantise_w1(1, "x_all"))

        pre = []
        for t in range(PACK):
            w1_codes, w1_scales = w1_q[t // 2]
            cols = slice(P * (t % 2), P * (t % 2 + 1))
            pieces = []
            for links in LINK_PIECES if t == FIRST_PLANE else (slice(0, S),):
                bank_name = "pre%d_%d" % (t, links.start)
                bank = psum.tile([P, links.stop - links.start], F32, name=bank_name, tag=bank_name)
                nc.tensor.matmul_mx(
                    out=bank[:],
                    lhsT=w1_codes[:, cols].bitcast(FP8X4),
                    lhsT_scale=w1_scales[:, cols],
                    rhs=x_pick[:, links].bitcast(FP8X4),
                    rhs_scale=xs_pick[:, links],
                    start=True,
                    stop=True,
                )
                pieces.append((links, bank))
            pre.append(pieces)

        w2_bf, w2_codes = {}, {}
        w2_scales = [keep.tile([P, W2_HALF], U8, name="w2_scales%d" % h, align_bytes=64) for h in range(2)]

        def round_w2(h, copy):
            w2_bf[h] = keep.tile([P, W2_HALF, PACK], BF16, name="w2_bf%d" % h, align_bytes=64)
            copy(
                out=w2_bf[h][:].rearrange("p (c i) j -> p c j i", i=LINE),
                in_=w2_raw[h][:].rearrange("p j (c i) -> p c j i", i=LINE),
            )

        def quantise_w2(h, tag):
            w2_codes[h] = keep.tile([P, W2_HALF], U32, name="w2_codes%d" % h, tag=tag, align_bytes=64)
            nc.vector.quantize_mx(
                out=w2_codes[h][:].bitcast(FP8X4),
                scales=w2_scales[h][:],
                in_=w2_bf[h][:].rearrange("p c j -> p (c j)"),
            )

        round_w2(0, nc.vector.tensor_copy)
        quantise_w2(0, "w2_codes0")

        z_pairs = [keep.tile([P, 2, V], BF16, name="z_pair%d" % u) for u in range(2)]
        y, y1, diff, prod = {}, {}, {}, {}

        def finish(t):
            nc.vector.scalar_tensor_tensor(
                z_pairs[t // 2][:, t % 2, :], diff[t][:], gn_sb[:, t : t + 1], prod[t][:], ALU.mult, ALU.mult
            )

        for t in range(PACK):
            y[t] = keep.tile([P, S], F32, name="y%d" % t)
            for links, bank in pre[t]:
                nc.scalar.activation(y[t][:, links], bank[:], ACT.Tanh)
            half4 = keep.tile([P, V], F32, name="half4_%d" % t)
            nc.scalar.activation(half4[:], y[t][:].indirect(l4[:]), ACT.Copy, scale=-0.5)
            y1[t] = keep.tile([P, V], F32, name="y1_%d" % t)
            diff[t] = keep.tile([P, V], F32, name="diff%d" % t)
            prod[t] = keep.tile([P, V], F32, name="prod%d" % t)
            if t == FIRST_PLANE:
                nc.vector.tensor_copy(y1[t][:], y[t][:].indirect(l1[:]))
            elif t != LATE_PLANE:
                nc.scalar.activation(y1[t][:], y[t][:].indirect(l1[:]), ACT.Copy)
            nc.vector.tensor_tensor(diff[t][:], y[t][:].indirect(l3[:]), half4[:], ALU.add)
            if t > 0 and t - 1 != LATE_PLANE:
                finish(t - 1)
            if t != LATE_PLANE:
                nc.vector.tensor_tensor(prod[t][:], y[t][:].indirect(l2[:]), y1[t][:], ALU.mult)

        late = LATE_PLANE
        nc.scalar.activation(y1[late][:], y[late][:].indirect(l1[:]), ACT.Copy)
        y2_late = keep.tile([P, V], F32, name="y2_late")
        nc.scalar.activation(y2_late[:], y[late][:].indirect(l2[:]), ACT.Copy)
        nc.vector.scalar_tensor_tensor(
            prod[late][:], diff[late][:], gn_sb[:, late : late + 1], y1[late][:], ALU.mult, ALU.mult
        )
        finish(PACK - 1)
        nc.vector.tensor_tensor(z_pairs[late // 2][:, late % 2, :], prod[late][:], y2_late[:], ALU.mult)

        z_bf = keep.tile([P, V, PACK], BF16, name="z_bf", tag="z_bf", align_bytes=64)
        for u, copy in enumerate((nc.scalar.copy, nc.vector.tensor_copy)):
            copy(out=z_bf[:, :, 2 * u : 2 * u + 2], in_=z_pairs[u][:].rearrange("p t v -> p v t"))
        round_w2(1, nc.scalar.copy)
        z_codes = keep.tile([P, V], U32, name="z_codes", align_bytes=64)
        z_scales = keep.tile([P, V], U8, name="z_scales", align_bytes=64)
        nc.vector.quantize_mx(
            out=z_codes[:].bitcast(FP8X4), scales=z_scales[:], in_=z_bf[:].rearrange("p v t -> p (v t)")
        )
        quantise_w2(1, "z_bf")

        out_rows = out.rearrange("(b p) v -> p b v", p=P)
        for b in range(N // P):
            h, i = divmod(b, W2_HALF // P)
            result = keep.tile([P, V], F32, name="result%d" % b)
            acc = psum.tile([P, V], F32, name="acc%d" % b, tag="pre%d_0" % b)
            cols = slice(P * i, P * (i + 1))
            nc.tensor.matmul_mx(
                out=acc[:],
                lhsT=w2_codes[h][:, cols].bitcast(FP8X4),
                lhsT_scale=w2_scales[h][:, cols],
                rhs=z_codes[:].bitcast(FP8X4),
                rhs_scale=z_scales[:],
                start=True,
                stop=True,
            )
            nc.vector.tensor_tensor(result[:], acc[:], res_sb[:, b, :], ALU.add)
            queue = nc.scalar if b % 2 == 0 else nc.sync
            queue.dma_start(out=out_rows[:, b, :], in_=result[:])
